import numpy as np
CORES = [4,5,6,7,0,1,2,3]
N = 8
def setup_inputs(rng):
    return {"x": rng.standard_normal((N, 128, 16), dtype=np.float32)}
def reference(x):
    p = 128 // N
    blocks = x.reshape(N, N, p, 16)
    return {"y": np.ascontiguousarray(blocks.transpose(1, 0, 2, 3)).reshape(N, 128, 16)}

from concourse.bass import DstId, RemoteDMATransfer

N = 8
ENG = 2

SCRATCH = {
    "send": ("dram", [N, 128, 2], "float32"),
    "recv": ("dram", [N, 128, 2], "float32"),
}
SEMAPHORES = ["loaded", "read", "arrived", "stored"]


def rank_program(g, core, T, topo):
    rank = T.rank_of(core)
    if rank is None:
        return
    p = 128 // N

    g.dma_start(T.send[:], T.x[:]).then_inc(T.sem.loaded, 16)
    g.dma_start(T.recv[rank], T.x[p * rank:p * (rank + 1), :]).then_inc(T.sem.loaded, 16)
    g.wait_ge(T.sem.loaded, 32)

    transfers = []
    for k, j in enumerate(j for j in range(N) if j != rank):
        rid, pid = topo.addr(T.cores[j])[:2]
        transfers.append(RemoteDMATransfer(
            dst_ids=[DstId(rid=rid, pnc=pid)],
            dma_engine_mask=((1 << ENG) - 1) << (ENG * k),
            remote_sem=T.sem.arrived,
            src=T.send[j],
            dst=T.recv[rank],
        ))
    g.remote_dma_fused(transfers, local_sem=T.sem.read)

    g.wait_ge(T.sem.arrived, ENG * (N - 1))
    g.dma_start(T.y[:], T.recv[:]).then_inc(T.sem.stored, 16)
    g.wait_ge(T.sem.stored, 16)
    g.wait_ge(T.sem.read, ENG * (N - 1))
